import numpy as np
import ml_dtypes


def mxq(x, axis, fmt="e4m3"):
    dtype, down = {"e4m3": (ml_dtypes.float8_e4m3fn, 7), "e5m2": (ml_dtypes.float8_e5m2, 14)}[fmt]
    v = np.moveaxis(np.asarray(x, np.float32).astype(ml_dtypes.bfloat16).astype(np.float64), axis, -1)
    blocks = v.reshape(v.shape[:-1] + (-1, 32))
    amax = np.abs(blocks).max(-1, keepdims=True)
    byte = np.maximum(np.where(amax > 0, np.frexp(amax)[1] - 1 + 127, 0) - down, 1)
    scale = np.exp2(byte - 127.0)
    codes = (blocks / scale).astype(np.float32).astype(dtype).astype(np.float64)
    return np.moveaxis((codes * scale).reshape(v.shape), -1, axis)


WIDE = False


def mx_kscale(k):
    if not WIDE:
        return np.ones(k)
    levels = np.array([10, -10, 5, -5, 0])
    if k % 512:
        return np.exp2(np.random.permutation(np.resize(levels, k // 32))).repeat(32)
    a = np.empty((k // 512, 16))
    for p in range(k // 512):
        a[p, :8] = np.random.permutation(np.resize(levels, 8))
        for g in range(8):
            far = levels[np.abs(levels - a[p, g]) >= 10]
            a[p, g + 8] = far[np.random.randint(len(far))]
    return np.exp2(a.ravel()).repeat(32)


def f64(x):
    return np.asarray(x).astype(np.float64)


def striped(idx):
    return np.tile(idx.reshape(-1, 16).T, (8, 1)).astype(np.uint16)


def unstriped(offs):
    return offs[:16].T.reshape(-1).astype(np.int64)


E2M1 = np.array([0.0, 0.5, 1.0, 1.5, 2.0, 3.0, 4.0, 6.0, -0.0, -0.5, -1.0, -1.5, -2.0, -3.0, -4.0, -6.0])


def pack_weight(w, fmt):
    k, n = w.shape
    w = f64(np.asarray(w, np.float32).astype(ml_dtypes.bfloat16)).reshape(k // 32, 32, n)
    amax = np.abs(w).max(1)
    if fmt == "e4m3":
        byte = np.frexp(amax)[1] - 1 + 127 - 7
    else:
        mant, ex = np.frexp(amax / 6.0)
        byte = np.where(mant > 0.5, ex, ex - 1) + 127
    byte = np.clip(np.where(amax > 0, byte, 1), 1, 254)
    scaled = (w * np.exp2(127.0 - byte)[:, None, :]).reshape(k, n).astype(np.float32)
    by_word = np.ascontiguousarray(scaled.reshape(k // 512, 128, 4, n).transpose(0, 1, 3, 2))
    if fmt == "e4m3":
        words = by_word.astype(ml_dtypes.float8_e4m3fn).view(np.uint8)
    else:
        c = by_word.astype(ml_dtypes.float4_e2m1fn).view(np.uint8) & 0xF
        words = (c[..., 0::2] | (c[..., 1::2] << 4)).reshape(k // 512, 128, 2 * n)
    return np.ascontiguousarray(words), np.ascontiguousarray(byte.astype(np.uint8).reshape(k // 512, 16, n))


def unpack_weight(words, scales, fmt):
    g, _, n = scales.shape
    words = np.ascontiguousarray(words).reshape(g, 128, n, -1)
    if fmt == "e4m3":
        vals = words.view(ml_dtypes.float8_e4m3fn).astype(np.float64)
    else:
        nib = np.empty((g, 128, n, 4), np.uint8)
        nib[..., 0::2] = words & 0xF
        nib[..., 1::2] = words >> 4
        vals = E2M1[nib]
    vals = vals * np.repeat(np.exp2(scales.astype(np.float64) - 127.0), 8, axis=1)[..., None]
    return vals.transpose(0, 1, 3, 2).reshape(g * 512, n)


def gelu(v):
    return 0.5 * v * (1.0 + np.tanh(np.sqrt(2.0 / np.pi) * (v + 0.044715 * v**3)))


K, H, N, T, S, T2 = 512, 1024, 768, 2048, 1024, 2048

def setup_inputs():
    n = np.random.standard_normal
    s = mx_kscale(K)[:, None]
    u = mx_kscale(H)[:, None]
    tab_words, tab_scales = pack_weight(n((K, T)) * s, "e4m3")
    wc_words, wc_scales = pack_weight(n((H, N)) / np.sqrt(H) / u, "e2m1")
    we_words, we_scales = pack_weight(1.3 * n((K, N)) / np.sqrt(K) / s, "e4m3")
    return {
        "tab_words": tab_words, "tab_scales": tab_scales,
        "offs": striped(np.random.permutation(T)[:S]),
        "offs2": striped(np.random.permutation(T)[:S]),
        "offs3": striped(np.random.permutation(T2)[:S]),
        "wa": (0.8 * n((K, H)) / np.sqrt(K) / s * u.T).astype(np.float32),
        "wb": (0.8 * n((K, H)) / np.sqrt(K) / s * u.T).astype(np.float32),
        "bh": (0.6 * n(H) * u[:, 0]).astype(np.float32),
        "wc_words": wc_words, "wc_scales": wc_scales,
        "wd": (n((K, N)) / np.sqrt(K) / s).astype(np.float32),
        "we_words": we_words, "we_scales": we_scales,
        "be": (0.5 * n(N)).astype(np.float32),
        "wgo": np.exp(0.3 * n((128, S))).astype(np.float32),
    }

def reference(tab_words, tab_scales, offs, offs2, offs3, wa, wb, bh, wc_words, wc_scales, wd, we_words, we_scales, be, wgo):
    TW = unpack_weight(tab_words, tab_scales, "e4m3")
    v = TW[:, unstriped(offs)]
    v2 = TW[:, unstriped(offs2)]
    d = mxq(f64(wa), 0, "e4m3").T @ v + mxq(-f64(wb), 0, "e4m3").T @ v2
    h = np.abs(d + f64(bh)[:, None])
    wc = unpack_weight(wc_words, wc_scales, "e2m1")
    we = unpack_weight(we_words, we_scales, "e4m3")
    e = wc.T @ mxq(h, 0, "e4m3") + mxq(f64(wd), 0, "e4m3").T @ v
    top = (we.T @ v2) + f64(be)[:, None]
    y = np.minimum(e, top)
    out = np.zeros((N, T2))
    out[:, unstriped(offs3)] = np.tile(f64(wgo), (N // 128, 1)) * y
    return out

@@ -1,0 +1,287 @@
+from contextlib import ExitStack
+
+import concourse.mybir as mybir
+
+K, H, N, T, S, T2 = 512, 1024, 768, 2048, 1024, 2048
+FLOPS = 2 * S * (2 * K * H + H * N + 2 * K * N)
+
+F32 = mybir.dt.float32
+BF16 = mybir.dt.bfloat16
+I32 = mybir.dt.int32
+U32 = mybir.dt.uint32
+U16 = mybir.dt.uint16
+U8 = mybir.dt.uint8
+FP8X4 = mybir.dt.float8_e4m3fn_x4
+FP4X4 = mybir.dt.float4_e2m1fn_x4
+ACT = mybir.ActivationFunctionType
+ALU = mybir.AluOpType
+
+P = 128
+PACK = 4
+K_PASS = P * PACK
+H_PASSES = H // K_PASS
+ROW_TILES = N // P
+CHUNK = 256
+ROUNDS = [slice(first, first + CHUNK) for first in range(0, S, CHUNK)]
+EARLY_PAGES = 4
+PAGE_BYTES = 4 * T2
+WD_COLS = 256
+BANK = 512
+HALVES = S // BANK
+SLOT_BYTES = 4096
+
+
+def tile_list_call_ring_scores_kernel(
+    tc, tab_words, tab_scales, offs, offs2, offs3, wa, wb, bh, wc_words, wc_scales, wd, we_words, we_scales, be, wgo, out
+):
+    nc = tc.nc
+    with ExitStack() as ctx:
+        keep = ctx.enter_context(tc.tile_pool(name="keep", bufs=1))
+        work = ctx.enter_context(tc.tile_pool(name="work", bufs=1))
+        late = ctx.enter_context(tc.tile_pool(name="late", bufs=1))
+        shared = ctx.enter_context(tc.tile_pool(name="shared", bufs=1))
+        psum = ctx.enter_context(tc.psum_pool(name="psum", bufs=1))
+
+        def held(shape, dtype, name):
+            return keep.tile(shape, dtype, name=name, align_bytes=64)
+
+        caller_list = held([P, S // 16], U16, "caller_list")
+        called_list = held([P, S // 16], U16, "called_list")
+        case_list = held([P, S // 16], U16, "case_list")
+        tab_w = held([P, T], U32, "tab_w")
+        tab_s = held([P, T], U8, "tab_s")
+        wc_w = held([P, H_PASSES, 2 * N], U8, "wc_w")
+        wc_s = held([P, H_PASSES, N], U8, "wc_s")
+        we_w = held([P, N], U32, "we_w")
+        we_s = held([P, N], U8, "we_s")
+        bh_sb = held([P, H_PASSES, PACK], F32, "bh_sb")
+        be_sb = held([P, ROW_TILES], F32, "be_sb")
+        wgo_sb = held([P, S], F32, "wgo_sb")
+        wa_raw = [held([P, PACK, K_PASS], F32, f"wa_raw{b}") for b in range(H_PASSES)]
+        wb_raw = [held([P, PACK, K_PASS], F32, f"wb_raw{b}") for b in range(H_PASSES)]
+        wd_raw = [held([P, PACK, WD_COLS], F32, f"wd_raw{i}") for i in range(N // WD_COLS)]
+        pages = [held([P, T2], F32, f"page{i}") for i in range(EARLY_PAGES)]
+
+        nc.vector.memset(tab_s[:].bitcast(I32), 0)
+        nc.gpsimd.memset(wc_s[:].rearrange("p a n -> p (a n)").bitcast(I32), 0)
+        nc.gpsimd.memset(we_s[:].bitcast(I32), 0)
+        for page in pages:
+            nc.gpsimd.memset(page[:], 0.0)
+
+        def load_rows(raw, w, first):
+            cols = raw.shape[2]
+            nc.sync.dma_start(raw[:], w[:, first : first + cols].rearrange("(p j) c -> p j c", j=PACK))
+
+        nc.sync.dma_start(caller_list[:], offs)
+        nc.sync.dma_start(tab_w[:].bitcast(I32), tab_words[0].rearrange("p t i -> p (t i)").bitcast(I32))
+        for q in range(4):
+            nc.sync.dma_start(tab_s[32 * q : 32 * q + 4, :].bitcast(I32), tab_scales[0, 4 * q : 4 * q + 4, :].bitcast(I32))
+        nc.sync.dma_start(called_list[:], offs2)
+        load_rows(wb_raw[0], wb, 0)
+        load_rows(wa_raw[0], wa, 0)
+        load_rows(wb_raw[1], wb, K_PASS)
+        nc.sync.dma_start(bh_sb[:], bh.rearrange("(b p t) -> p b t", p=P, t=PACK))
+        load_rows(wa_raw[1], wa, K_PASS)
+        load_rows(wd_raw[0], wd, 0)
+        nc.sync.dma_start(we_w[:].bitcast(I32), we_words[0].rearrange("p n i -> p (n i)").bitcast(I32))
+        for q in range(4):
+            nc.sync.dma_start(we_s[32 * q : 32 * q + 4, :].bitcast(I32), we_scales[0, 4 * q : 4 * q + 4, :].bitcast(I32))
+        with nc.allow_non_contiguous_dma(reason="one bias value for each partition and row tile"):
+            nc.sync.dma_start(be_sb[:], be.rearrange("(m p) -> p m", p=P))
+        nc.sync.dma_start(wc_w[:].bitcast(I32), wc_words.rearrange("a p n -> p a n").bitcast(I32))
+        for q in range(4):
+            nc.sync.dma_start(
+                wc_s[32 * q : 32 * q + 4, :, :].bitcast(I32),
+                wc_scales[:, 4 * q : 4 * q + 4, :].rearrange("a r n -> r a n").bitcast(I32),
+            )
+        nc.sync.dma_start(case_list[:], offs3)
+        nc.sync.dma_start(wgo_sb[:], wgo)
+        load_rows(wd_raw[1], wd, WD_COLS)
+        load_rows(wd_raw[2], wd, 2 * WD_COLS)
+
+        def gather(dst, window, lst, half):
+            cols = BANK // 16
+            nc.vector.tensor_copy(dst[:], window[:].indirect(lst[:, half * cols : (half + 1) * cols]))
+
+        def reused(shape, dtype, name, slot):
+            return shared.tile(shape, dtype, name=name, align_bytes=64, offset=slot * SLOT_BYTES)
+
+        caller_w = [held([P, BANK], U32, f"caller_w{i}") for i in range(HALVES)]
+        called_w = [held([P, BANK], U32, "called_w0")]
+        caller_s = [held([P, BANK], U8, "caller_s0")]
+        called_s = [held([P, BANK], U8, "called_s0")]
+        gather(caller_w[0], tab_w, caller_list, 0)
+        gather(called_w[0], tab_w, called_list, 0)
+        gather(caller_s[0], tab_s, caller_list, 0)
+        gather(called_s[0], tab_s, called_list, 0)
+        gather(caller_w[1], tab_w, caller_list, 1)
+
+        def gather_late(tiles, dtype, name, slot, window, lst):
+            tiles.append(reused([P, BANK], dtype, name, slot))
+            gather(tiles[1], window, lst, 1)
+
+        def picked(words, scales, cols):
+            half, first = divmod(cols.start, BANK)
+            inside = slice(first, first + cols.stop - cols.start)
+            return dict(rhs=words[half][:, inside].bitcast(FP8X4), rhs_scale=scales[half][:, inside])
+
+        def quantise(rounded, name):
+            words = rounded.shape[1] // PACK
+            codes = held([P, words], U32, name + "_w")
+            scales = held([P, words], U8, name + "_s")
+            nc.vector.quantize_mx(out=codes[:].bitcast(FP8X4), scales=scales[:], in_=rounded[:])
+            return codes, scales
+
+        def dealt_views(raw, rounded):
+            return (
+                rounded[:].rearrange("p (t m j) -> p m j t", t=PACK, j=PACK),
+                raw[:].rearrange("p j (m t) -> p m j t", t=PACK),
+            )
+
+        wa_q, wb_q = [], []
+        for b in range(H_PASSES):
+            rounded = held([P, PACK * K_PASS], BF16, f"wb_bf{b}")
+            nc.scalar.activation(*dealt_views(wb_raw[b], rounded), ACT.Copy, scale=-1.0)
+            wb_q.append(quantise(rounded, f"wb_q{b}"))
+            if b == 0:
+                rounded = reused([P, PACK * K_PASS], BF16, "wa_bf0", 0)
+                nc.scalar.copy(*dealt_views(wa_raw[b], rounded))
+            else:
+                rounded = held([P, PACK * K_PASS], BF16, "wa_bf1")
+                nc.vector.tensor_copy(*dealt_views(wa_raw[b], rounded))
+            wa_q.append(quantise(rounded, f"wa_q{b}"))
+            if b == 0:
+                gather_late(called_w, U32, "called_w1", 0, tab_w, called_list)
+
+        def round_wd(i, copy):
+            rounded = held([P, PACK * WD_COLS], BF16, f"wd_bf{i}")
+            copy(
+                rounded[:].rearrange("p (c i j) -> p c j i", i=4, j=PACK),
+                wd_raw[i][:].rearrange("p j (c i) -> p c j i", i=4),
+            )
+            return quantise(rounded, f"wd_q{i}")
+
+        h_w = [held([P, S], U32, f"h_w{b}") for b in range(H_PASSES)]
+        h_s = [held([P, S], U8, f"h_s{b}") for b in range(H_PASSES)]
+        h_woven = [[reused([P, PACK * CHUNK], BF16, f"h_woven0{b}", 1 + b) for b in range(H_PASSES)]]
+        for c in range(1, len(ROUNDS)):
+            width = ROUNDS[c].stop - ROUNDS[c].start
+            h_woven.append([held([P, PACK * width], BF16, f"h_woven{c}{b}") for b in range(H_PASSES)])
+        h_flat = held([P, PACK * CHUNK], BF16, "h_flat")
+
+        def make_h(c):
+            cols = ROUNDS[c]
+            width = cols.stop - cols.start
+            flat = h_flat[:, 0 : PACK * width].rearrange("p (t n) -> p t n", t=PACK)
+            per_bank = BANK // width
+            for b in range(H_PASSES):
+                for first_t in range(0, PACK, per_bank):
+                    d = psum.tile([P, per_bank, width], F32, name="d", bufs=4)
+                    for u in range(per_bank):
+                        m_cols = slice((first_t + u) * P, (first_t + u + 1) * P)
+                        for (w, s), gw, gs, first in ((wa_q[b], caller_w, caller_s, True), (wb_q[b], called_w, called_s, False)):
+                            nc.tensor.matmul_mx(
+                                out=d[:, u, :],
+                                lhsT=w[:, m_cols].bitcast(FP8X4),
+                                lhsT_scale=s[:, m_cols],
+                                **picked(gw, gs, cols),
+                                start=first,
+                                stop=not first,
+                            )
+                    for u in range(per_bank):
+                        t = first_t + u
+                        nc.scalar.activation(flat[:, t, :], d[:, u, :], ACT.Abs, bias=bh_sb[:, b, t : t + 1])
+                weave = nc.vector.tensor_copy if c == 0 else nc.scalar.copy
+                weave(
+                    h_woven[c][b][:].rearrange("p (c i t) -> p c t i", i=4, t=PACK),
+                    flat.rearrange("p t (c i) -> p c t i", i=4),
+                )
+                nc.vector.quantize_mx(out=h_w[b][:, cols].bitcast(FP8X4), scales=h_s[b][:, cols], in_=h_woven[c][b][:])
+
+        def scores(parts, y, ceiling, e, order):
+            spans, first = [], 0
+            for m, cols in parts:
+                width = cols.stop - cols.start
+                spans.append((m, cols, slice(m * P, (m + 1) * P), slice(first, first + width)))
+                first = first + width
+            top = psum.tile([P, BANK], F32, name="top", bufs=2)
+            for m, cols, n_cols, span in spans:
+                nc.tensor.matmul_mx(
+                    out=top[:, span],
+                    lhsT=we_w[:, n_cols].bitcast(FP8X4),
+                    lhsT_scale=we_s[:, n_cols],
+                    **picked(called_w, called_s, cols),
+                    start=True,
+                    stop=True,
+                )
+            for m, cols, n_cols, span in spans:
+                nc.scalar.activation(ceiling[:, span], top[:, span], ACT.Identity, bias=be_sb[:, m : m + 1])
+            passes = []
+            for source in order:
+                for m, cols, n_cols, span in spans:
+                    if source == "wd":
+                        wd_w, wd_s = wd_q[m * P // WD_COLS]
+                        wd_cols = slice(m * P % WD_COLS, m * P % WD_COLS + P)
+                        operands = dict(
+                            lhsT=wd_w[:, wd_cols].bitcast(FP8X4),
+                            lhsT_scale=wd_s[:, wd_cols],
+                            **picked(caller_w, caller_s, cols),
+                        )
+                    else:
+                        operands = dict(
+                            lhsT=wc_w[:, source, 2 * m * P : 2 * (m + 1) * P].bitcast(FP4X4),
+                            lhsT_scale=wc_s[:, source, n_cols],
+                            rhs=h_w[source][:, cols].bitcast(FP8X4),
+                            rhs_scale=h_s[source][:, cols],
+                        )
+                    passes.append((span, operands))
+            for i, (span, operands) in enumerate(passes):
+                nc.tensor.matmul_mx(out=e[:, span], start=i == 0, stop=i == len(passes) - 1, **operands)
+            nc.vector.tensor_tensor(y, e[:], ceiling[:], ALU.min)
+
+        def place(m, cols, y):
+            nc.vector.tensor_tensor(
+                pages[m][:].indirect(case_list[:, cols.start // 16 : cols.stop // 16]), y, wgo_sb[:, cols], ALU.mult
+            )
+
+        def store(m):
+            nc.sync.dma_start(out[m * P : (m + 1) * P, :], pages[m][:])
+
+        wd_q = [round_wd(0, nc.scalar.copy)]
+        make_h(0)
+        gather_late(caller_s, U8, "caller_s1", 1, tab_s, caller_list)
+        gather_late(called_s, U8, "called_s1", 2, tab_s, called_list)
+        for c, cols in enumerate(ROUNDS):
+            tiles = ROW_TILES if cols.stop <= BANK else EARLY_PAGES
+            for m in range(0, tiles, 2):
+                late_offset = m // 2 * PAGE_BYTES
+                if c == 0 and m > 0:
+                    wd_q.append(round_wd(m // 2, nc.scalar.copy))
+                if m == tiles - 2 and c + 1 < len(ROUNDS):
+                    make_h(c + 1)
+                    y = h_woven[c + 1][H_PASSES - 1][:].bitcast(F32)
+                else:
+                    y_tile = work.tile([P, BANK], F32, name="y_tile", bufs=3)
+                    y = y_tile[:]
+                if c == 0 and m < EARLY_PAGES:
+                    ceiling = late.tile([P, BANK], F32, name=f"first_ceiling{m}", offset=late_offset)
+                else:
+                    ceiling = held([P, BANK], F32, f"ceiling{c}{m}")
+                e = psum.tile([P, BANK], F32, name="e", bufs=2)
+                scores([(m, cols), (m + 1, cols)], y, ceiling, e, ("wd", 0, 1) if (c, m) == (0, 0) else (1, 0, "wd"))
+                if c == 0 and m < EARLY_PAGES:
+                    pages.append(late.tile([P, T2], F32, name=f"late_page{m}", offset=late_offset))
+                    nc.gpsimd.memset(pages[-1][:], 0.0)
+                for u in range(2):
+                    place(m + u, cols, y[:, u * CHUNK : (u + 1) * CHUNK])
+                    if c == len(ROUNDS) - 1:
+                        store(m + u)
+
+        cols = slice(BANK, S)
+        for m in range(EARLY_PAGES, ROW_TILES):
+            y_tile = work.tile([P, BANK], F32, name="y_tile", bufs=3)
+            ceiling = held([P, BANK], F32, f"ceiling_wide{m}")
+            e = psum.tile([P, BANK], F32, name="d", bufs=4)
+            scores([(m, cols)], y_tile[:], ceiling, e, (1, 0, "wd"))
+            place(m, cols, y_tile[:])
+            store(m)

@@ -21,11 +21,8 @@ PACK = 4
 K_PASS = P * PACK
 H_PASSES = H // K_PASS
 ROW_TILES = N // P
-CHUNK = 256
-ROUNDS = [slice(first, first + CHUNK) for first in range(0, S, CHUNK)]
-EARLY_PAGES = 4
-PAGE_BYTES = 4 * T2
-WD_COLS = 256
+PAGES = 3
+WD_EARLY = 512
 BANK = 512
 HALVES = S // BANK
 SLOT_BYTES = 4096
@@ -38,7 +35,6 @@ def tile_list_call_ring_scores_kernel(
     with ExitStack() as ctx:
         keep = ctx.enter_context(tc.tile_pool(name="keep", bufs=1))
         work = ctx.enter_context(tc.tile_pool(name="work", bufs=1))
-        late = ctx.enter_context(tc.tile_pool(name="late", bufs=1))
         shared = ctx.enter_context(tc.tile_pool(name="shared", bufs=1))
         psum = ctx.enter_context(tc.psum_pool(name="psum", bufs=1))
 
@@ -59,14 +55,14 @@ def tile_list_call_ring_scores_kernel(
         wgo_sb = held([P, S], F32, "wgo_sb")
         wa_raw = [held([P, PACK, K_PASS], F32, f"wa_raw{b}") for b in range(H_PASSES)]
         wb_raw = [held([P, PACK, K_PASS], F32, f"wb_raw{b}") for b in range(H_PASSES)]
-        wd_raw = [held([P, PACK, WD_COLS], F32, f"wd_raw{i}") for i in range(N // WD_COLS)]
-        pages = [held([P, T2], F32, f"page{i}") for i in range(EARLY_PAGES)]
+        wd_raw = [held([P, PACK, WD_EARLY], F32, "wd_raw0"), held([P, PACK, N - WD_EARLY], F32, "wd_raw1")]
+        pages = [held([P, T2], F32, f"page{i}") for i in range(PAGES)]
 
         nc.vector.memset(tab_s[:].bitcast(I32), 0)
-        nc.gpsimd.memset(wc_s[:].rearrange("p a n -> p (a n)").bitcast(I32), 0)
-        nc.gpsimd.memset(we_s[:].bitcast(I32), 0)
+        nc.vector.memset(wc_s[:].rearrange("p a n -> p (a n)").bitcast(I32), 0)
+        nc.vector.memset(we_s[:].bitcast(I32), 0)
         for page in pages:
-            nc.gpsimd.memset(page[:], 0.0)
+            nc.vector.memset(page[:].bitcast(I32), 0)
 
         def load_rows(raw, w, first):
             cols = raw.shape[2]
@@ -96,8 +92,7 @@ def tile_list_call_ring_scores_kernel(
             )
         nc.sync.dma_start(case_list[:], offs3)
         nc.sync.dma_start(wgo_sb[:], wgo)
-        load_rows(wd_raw[1], wd, WD_COLS)
-        load_rows(wd_raw[2], wd, 2 * WD_COLS)
+        load_rows(wd_raw[1], wd, WD_EARLY)
 
         def gather(dst, window, lst, half):
             cols = BANK // 16
@@ -119,11 +114,6 @@ def tile_list_call_ring_scores_kernel(
         def gather_late(tiles, dtype, name, slot, window, lst):
             tiles.append(reused([P, BANK], dtype, name, slot))
             gather(tiles[1], window, lst, 1)
-
-        def picked(words, scales, cols):
-            half, first = divmod(cols.start, BANK)
-            inside = slice(first, first + cols.stop - cols.start)
-            return dict(rhs=words[half][:, inside].bitcast(FP8X4), rhs_scale=scales[half][:, inside])
 
         def quantise(rounded, name):
             words = rounded.shape[1] // PACK
@@ -153,9 +143,8 @@ def tile_list_call_ring_scores_kernel(
             if b == 0:
                 gather_late(called_w, U32, "called_w1", 0, tab_w, called_list)
 
-        def round_wd(i, copy):
-            rounded = held([P, PACK * WD_COLS], BF16, f"wd_bf{i}")
-            copy(
+        def round_wd(i, rounded):
+            nc.scalar.copy(
                 rounded[:].rearrange("p (c i j) -> p c j i", i=4, j=PACK),
                 wd_raw[i][:].rearrange("p j (c i) -> p c j i", i=4),
             )
@@ -163,125 +152,129 @@ def tile_list_call_ring_scores_kernel(
 
         h_w = [held([P, S], U32, f"h_w{b}") for b in range(H_PASSES)]
         h_s = [held([P, S], U8, f"h_s{b}") for b in range(H_PASSES)]
-        h_woven = [[reused([P, PACK * CHUNK], BF16, f"h_woven0{b}", 1 + b) for b in range(H_PASSES)]]
-        for c in range(1, len(ROUNDS)):
-            width = ROUNDS[c].stop - ROUNDS[c].start
-            h_woven.append([held([P, PACK * width], BF16, f"h_woven{c}{b}") for b in range(H_PASSES)])
-        h_flat = held([P, PACK * CHUNK], BF16, "h_flat")
+        h_woven = [
+            [reused([P, PACK * BANK], BF16, f"h_woven{half}{b}", 1 + H_PASSES * half + b) for b in range(H_PASSES)]
+            for half in range(HALVES)
+        ]
+        h_flat = [held([P, PACK, BANK], BF16, f"h_flat{b}") for b in range(H_PASSES)]
 
-        def make_h(c):
-            cols = ROUNDS[c]
-            width = cols.stop - cols.start
-            flat = h_flat[:, 0 : PACK * width].rearrange("p (t n) -> p t n", t=PACK)
-            per_bank = BANK // width
+        def weave(copy, woven, flat):
+            copy(
+                woven[:].rearrange("p (c i t) -> p c t i", i=4, t=PACK),
+                flat[:].rearrange("p t (c i) -> p c t i", i=4),
+            )
+
+        def make_h(half):
+            cols = slice(half * BANK, (half + 1) * BANK)
             for b in range(H_PASSES):
-                for first_t in range(0, PACK, per_bank):
-                    d = psum.tile([P, per_bank, width], F32, name="d", bufs=4)
-                    for u in range(per_bank):
-                        m_cols = slice((first_t + u) * P, (first_t + u + 1) * P)
-                        for (w, s), gw, gs, first in ((wa_q[b], caller_w, caller_s, True), (wb_q[b], called_w, called_s, False)):
-                            nc.tensor.matmul_mx(
-                                out=d[:, u, :],
-                                lhsT=w[:, m_cols].bitcast(FP8X4),
-                                lhsT_scale=s[:, m_cols],
-                                **picked(gw, gs, cols),
-                                start=first,
-                                stop=not first,
-                            )
-                    for u in range(per_bank):
-                        t = first_t + u
-                        nc.scalar.activation(flat[:, t, :], d[:, u, :], ACT.Abs, bias=bh_sb[:, b, t : t + 1])
-                weave = nc.vector.tensor_copy if c == 0 else nc.scalar.copy
-                weave(
-                    h_woven[c][b][:].rearrange("p (c i t) -> p c t i", i=4, t=PACK),
-                    flat.rearrange("p t (c i) -> p c t i", i=4),
-                )
-                nc.vector.quantize_mx(out=h_w[b][:, cols].bitcast(FP8X4), scales=h_s[b][:, cols], in_=h_woven[c][b][:])
+                for t in range(PACK):
+                    d = psum.tile([P, BANK], F32, name="d", bufs=4)
+                    m_cols = slice(t * P, (t + 1) * P)
+                    for (w, s), gw, gs, first in ((wa_q[b], caller_w, caller_s, True), (wb_q[b], called_w, called_s, False)):
+                        nc.tensor.matmul_mx(
+                            out=d[:],
+                            lhsT=w[:, m_cols].bitcast(FP8X4),
+                            lhsT_scale=s[:, m_cols],
+                            rhs=gw[half][:].bitcast(FP8X4),
+                            rhs_scale=gs[half][:],
+                            start=first,
+                            stop=not first,
+                        )
+                    nc.scalar.activation(h_flat[b][:, t, :], d[:], ACT.Abs, bias=bh_sb[:, b, t : t + 1])
+                woven = h_woven[half][b]
+                weave(nc.vector.tensor_copy if half == 0 else nc.scalar.copy, woven, h_flat[b])
+                nc.vector.quantize_mx(out=h_w[b][:, cols].bitcast(FP8X4), scales=h_s[b][:, cols], in_=woven[:])
 
-        def scores(parts, y, ceiling, e, order):
-            spans, first = [], 0
-            for m, cols in parts:
-                width = cols.stop - cols.start
-                spans.append((m, cols, slice(m * P, (m + 1) * P), slice(first, first + width)))
-                first = first + width
-            top = psum.tile([P, BANK], F32, name="top", bufs=2)
-            for m, cols, n_cols, span in spans:
-                nc.tensor.matmul_mx(
-                    out=top[:, span],
-                    lhsT=we_w[:, n_cols].bitcast(FP8X4),
-                    lhsT_scale=we_s[:, n_cols],
-                    **picked(called_w, called_s, cols),
-                    start=True,
-                    stop=True,
+        ceilings = {}
+
+        def make_ceiling(m, half):
+            n_cols = slice(m * P, (m + 1) * P)
+            top = psum.tile([P, BANK], F32, name="top", bufs=1)
+            nc.tensor.matmul_mx(
+                out=top[:],
+                lhsT=we_w[:, n_cols].bitcast(FP8X4),
+                lhsT_scale=we_s[:, n_cols],
+                rhs=called_w[half][:].bitcast(FP8X4),
+                rhs_scale=called_s[half][:],
+                start=True,
+                stop=True,
+            )
+            ceiling = held([P, BANK], F32, f"ceiling{m}{half}")
+            nc.scalar.activation(ceiling[:], top[:], ACT.Identity, bias=be_sb[:, m : m + 1])
+            ceilings[m, half] = ceiling
+
+        def scores(m, half, y, wd_place):
+            cols = slice(half * BANK, (half + 1) * BANK)
+            n_cols = slice(m * P, (m + 1) * P)
+            if (m, half) not in ceilings:
+                make_ceiling(m, half)
+            e = psum.tile([P, BANK], F32, name="e", bufs=3)
+            wd_w, wd_s = wd_q[m * P // WD_EARLY]
+            wd_cols = slice(m * P % WD_EARLY, m * P % WD_EARLY + P)
+            passes = [
+                (
+                    wc_w[:, b, 2 * m * P : 2 * (m + 1) * P].bitcast(FP4X4),
+                    wc_s[:, b, n_cols],
+                    h_w[b][:, cols].bitcast(FP8X4),
+                    h_s[b][:, cols],
                 )
-            for m, cols, n_cols, span in spans:
-                nc.scalar.activation(ceiling[:, span], top[:, span], ACT.Identity, bias=be_sb[:, m : m + 1])
-            passes = []
-            for source in order:
-                for m, cols, n_cols, span in spans:
-                    if source == "wd":
-                        wd_w, wd_s = wd_q[m * P // WD_COLS]
-                        wd_cols = slice(m * P % WD_COLS, m * P % WD_COLS + P)
-                        operands = dict(
-                            lhsT=wd_w[:, wd_cols].bitcast(FP8X4),
-                            lhsT_scale=wd_s[:, wd_cols],
-                            **picked(caller_w, caller_s, cols),
-                        )
-                    else:
-                        operands = dict(
-                            lhsT=wc_w[:, source, 2 * m * P : 2 * (m + 1) * P].bitcast(FP4X4),
-                            lhsT_scale=wc_s[:, source, n_cols],
-                            rhs=h_w[source][:, cols].bitcast(FP8X4),
-                            rhs_scale=h_s[source][:, cols],
-                        )
-                    passes.append((span, operands))
-            for i, (span, operands) in enumerate(passes):
-                nc.tensor.matmul_mx(out=e[:, span], start=i == 0, stop=i == len(passes) - 1, **operands)
-            nc.vector.tensor_tensor(y, e[:], ceiling[:], ALU.min)
+                for b in range(H_PASSES)
+            ]
+            wd_pass = (
+                wd_w[:, wd_cols].bitcast(FP8X4),
+                wd_s[:, wd_cols],
+                caller_w[half][:].bitcast(FP8X4),
+                caller_s[half][:],
+            )
+            passes.insert(wd_place, wd_pass)
+            for i, (lhsT, lhsT_scale, rhs, rhs_scale) in enumerate(passes):
+                nc.tensor.matmul_mx(
+                    out=e[:],
+                    lhsT=lhsT,
+                    lhsT_scale=lhsT_scale,
+                    rhs=rhs,
+                    rhs_scale=rhs_scale,
+                    start=i == 0,
+                    stop=i == len(passes) - 1,
+                )
+            nc.vector.tensor_tensor(y, e[:], ceilings[m, half][:], ALU.min)
 
         def place(m, cols, y):
             nc.vector.tensor_tensor(
-                pages[m][:].indirect(case_list[:, cols.start // 16 : cols.stop // 16]), y, wgo_sb[:, cols], ALU.mult
+                pages[m % PAGES][:].indirect(case_list[:, cols.start // 16 : cols.stop // 16]), y, wgo_sb[:, cols], ALU.mult
             )
 
         def store(m):
-            nc.sync.dma_start(out[m * P : (m + 1) * P, :], pages[m][:])
+            nc.sync.dma_start(out[m * P : (m + 1) * P, :], pages[m % PAGES][:])
 
-        wd_q = [round_wd(0, nc.scalar.copy)]
         make_h(0)
+        wd_q = [round_wd(0, held([P, PACK * WD_EARLY], BF16, "wd_bf0"))]
         gather_late(caller_s, U8, "caller_s1", 1, tab_s, caller_list)
         gather_late(called_s, U8, "called_s1", 2, tab_s, called_list)
-        for c, cols in enumerate(ROUNDS):
-            tiles = ROW_TILES if cols.stop <= BANK else EARLY_PAGES
-            for m in range(0, tiles, 2):
-                late_offset = m // 2 * PAGE_BYTES
-                if c == 0 and m > 0:
-                    wd_q.append(round_wd(m // 2, nc.scalar.copy))
-                if m == tiles - 2 and c + 1 < len(ROUNDS):
-                    make_h(c + 1)
-                    y = h_woven[c + 1][H_PASSES - 1][:].bitcast(F32)
-                else:
-                    y_tile = work.tile([P, BANK], F32, name="y_tile", bufs=3)
-                    y = y_tile[:]
-                if c == 0 and m < EARLY_PAGES:
-                    ceiling = late.tile([P, BANK], F32, name=f"first_ceiling{m}", offset=late_offset)
-                else:
-                    ceiling = held([P, BANK], F32, f"ceiling{c}{m}")
-                e = psum.tile([P, BANK], F32, name="e", bufs=2)
-                scores([(m, cols), (m + 1, cols)], y, ceiling, e, ("wd", 0, 1) if (c, m) == (0, 0) else (1, 0, "wd"))
-                if c == 0 and m < EARLY_PAGES:
-                    pages.append(late.tile([P, T2], F32, name=f"late_page{m}", offset=late_offset))
-                    nc.gpsimd.memset(pages[-1][:], 0.0)
-                for u in range(2):
-                    place(m + u, cols, y[:, u * CHUNK : (u + 1) * CHUNK])
-                    if c == len(ROUNDS) - 1:
-                        store(m + u)
 
-        cols = slice(BANK, S)
-        for m in range(EARLY_PAGES, ROW_TILES):
-            y_tile = work.tile([P, BANK], F32, name="y_tile", bufs=3)
-            ceiling = held([P, BANK], F32, f"ceiling_wide{m}")
-            e = psum.tile([P, BANK], F32, name="d", bufs=4)
-            scores([(m, cols)], y_tile[:], ceiling, e, (1, 0, "wd"))
-            place(m, cols, y_tile[:])
+        def page_round(half):
+            cols = slice(half * BANK, (half + 1) * BANK)
+            ys = []
+            for m in range(PAGES + 1):
+                if m < PAGES:
+                    ys.append(work.tile([P, BANK], F32, name="y_half", bufs=3))
+                    scores(m, half, ys[m][:], 1)
+                if m > 0:
+                    place(m - 1, cols, ys[m - 1][:])
+                    if half == HALVES - 1:
+                        store(m - 1)
+
+        page_round(0)
+        make_h(1)
+        y_rows = {PAGES: h_woven[1][1][:].bitcast(F32)}
+        scores(PAGES, 0, y_rows[PAGES][:, 0:BANK], 0)
+        page_round(1)
+        wd_q.append(round_wd(1, h_flat[1][:].rearrange("p t n -> p (t n)")[:, 0 : PACK * (N - WD_EARLY)]))
+        scores(PAGES, 1, y_rows[PAGES][:, BANK:S], 1)
+        for m in range(PAGES, ROW_TILES):
+            if m + 1 < ROW_TILES:
+                y_rows[m + 1] = held([P, S], F32, f"y_row{m + 1}")[:]
+                for half in range(HALVES):
+                    scores(m + 1, half, y_rows[m + 1][:, half * BANK : (half + 1) * BANK], 0)
+            place(m, slice(0, S), y_rows[m])
             store(m)

@@ -203,7 +203,7 @@ def tile_list_call_ring_scores_kernel(
             nc.scalar.activation(ceiling[:], top[:], ACT.Identity, bias=be_sb[:, m : m + 1])
             ceilings[m, half] = ceiling
 
-        def scores(m, half, y, wd_place):
+        def scores(m, half, y, order):
             cols = slice(half * BANK, (half + 1) * BANK)
             n_cols = slice(m * P, (m + 1) * P)
             if (m, half) not in ceilings:
@@ -226,8 +226,8 @@ def tile_list_call_ring_scores_kernel(
                 caller_w[half][:].bitcast(FP8X4),
                 caller_s[half][:],
             )
-            passes.insert(wd_place, wd_pass)
-            for i, (lhsT, lhsT_scale, rhs, rhs_scale) in enumerate(passes):
+            passes.append(wd_pass)
+            for i, (lhsT, lhsT_scale, rhs, rhs_scale) in enumerate([passes[k] for k in order]):
                 nc.tensor.matmul_mx(
                     out=e[:],
                     lhsT=lhsT,
@@ -258,7 +258,7 @@ def tile_list_call_ring_scores_kernel(
             for m in range(PAGES + 1):
                 if m < PAGES:
                     ys.append(work.tile([P, BANK], F32, name="y_half", bufs=3))
-                    scores(m, half, ys[m][:], 1)
+                    scores(m, half, ys[m][:], (0, 2, 1) if half == 0 else (2, 1, 0) if m == 0 else (1, 0, 2))
                 if m > 0:
                     place(m - 1, cols, ys[m - 1][:])
                     if half == HALVES - 1:
@@ -267,14 +267,14 @@ def tile_list_call_ring_scores_kernel(
         page_round(0)
         make_h(1)
         y_rows = {PAGES: h_woven[1][1][:].bitcast(F32)}
-        scores(PAGES, 0, y_rows[PAGES][:, 0:BANK], 0)
+        scores(PAGES, 0, y_rows[PAGES][:, 0:BANK], (2, 0, 1))
         page_round(1)
         wd_q.append(round_wd(1, h_flat[1][:].rearrange("p t n -> p (t n)")[:, 0 : PACK * (N - WD_EARLY)]))
-        scores(PAGES, 1, y_rows[PAGES][:, BANK:S], 1)
+        scores(PAGES, 1, y_rows[PAGES][:, BANK:S], (1, 0, 2))
         for m in range(PAGES, ROW_TILES):
             if m + 1 < ROW_TILES:
                 y_rows[m + 1] = held([P, S], F32, f"y_row{m + 1}")[:]
                 for half in range(HALVES):
-                    scores(m + 1, half, y_rows[m + 1][:, half * BANK : (half + 1) * BANK], 0)
+                    scores(m + 1, half, y_rows[m + 1][:, half * BANK : (half + 1) * BANK], (2, 0, 1))
             place(m, slice(0, S), y_rows[m])
             store(m)

from contextlib import ExitStack

import concourse.mybir as mybir

K, H, N, T, S, T2 = 512, 1024, 768, 2048, 1024, 2048
FLOPS = 2 * S * (2 * K * H + H * N + 2 * K * N)

F32 = mybir.dt.float32
BF16 = mybir.dt.bfloat16
I32 = mybir.dt.int32
U32 = mybir.dt.uint32
U16 = mybir.dt.uint16
U8 = mybir.dt.uint8
FP8X4 = mybir.dt.float8_e4m3fn_x4
FP4X4 = mybir.dt.float4_e2m1fn_x4
ACT = mybir.ActivationFunctionType
ALU = mybir.AluOpType

P = 128
PACK = 4
K_PASS = P * PACK
H_PASSES = H // K_PASS
ROW_TILES = N // P
PAGES = 3
WD_EARLY = 512
BANK = 512
HALVES = S // BANK
SLOT_BYTES = 4096


def tile_list_call_ring_scores_kernel(
    tc, tab_words, tab_scales, offs, offs2, offs3, wa, wb, bh, wc_words, wc_scales, wd, we_words, we_scales, be, wgo, out
):
    nc = tc.nc
    with ExitStack() as ctx:
        keep = ctx.enter_context(tc.tile_pool(name="keep", bufs=1))
        work = ctx.enter_context(tc.tile_pool(name="work", bufs=1))
        shared = ctx.enter_context(tc.tile_pool(name="shared", bufs=1))
        psum = ctx.enter_context(tc.psum_pool(name="psum", bufs=1))

        def held(shape, dtype, name):
            return keep.tile(shape, dtype, name=name, align_bytes=64)

        caller_list = held([P, S // 16], U16, "caller_list")
        called_list = held([P, S // 16], U16, "called_list")
        case_list = held([P, S // 16], U16, "case_list")
        tab_w = held([P, T], U32, "tab_w")
        tab_s = held([P, T], U8, "tab_s")
        wc_w = held([P, H_PASSES, 2 * N], U8, "wc_w")
        wc_s = held([P, H_PASSES, N], U8, "wc_s")
        we_w = held([P, N], U32, "we_w")
        we_s = held([P, N], U8, "we_s")
        bh_sb = held([P, H_PASSES, PACK], F32, "bh_sb")
        be_sb = held([P, ROW_TILES], F32, "be_sb")
        wgo_sb = held([P, S], F32, "wgo_sb")
        wa_raw = [held([P, PACK, K_PASS], F32, f"wa_raw{b}") for b in range(H_PASSES)]
        wb_raw = [held([P, PACK, K_PASS], F32, f"wb_raw{b}") for b in range(H_PASSES)]
        wd_raw = [held([P, PACK, WD_EARLY], F32, "wd_raw0"), held([P, PACK, N - WD_EARLY], F32, "wd_raw1")]
        pages = [held([P, T2], F32, f"page{i}") for i in range(PAGES)]

        nc.vector.memset(tab_s[:].bitcast(I32), 0)
        nc.vector.memset(wc_s[:].rearrange("p a n -> p (a n)").bitcast(I32), 0)
        nc.vector.memset(we_s[:].bitcast(I32), 0)
        for page in pages:
            nc.vector.memset(page[:].bitcast(I32), 0)

        def load_rows(raw, w, first):
            cols = raw.shape[2]
            nc.sync.dma_start(raw[:], w[:, first : first + cols].rearrange("(p j) c -> p j c", j=PACK))

        nc.sync.dma_start(caller_list[:], offs)
        nc.sync.dma_start(tab_w[:].bitcast(I32), tab_words[0].rearrange("p t i -> p (t i)").bitcast(I32))
        for q in range(4):
            nc.sync.dma_start(tab_s[32 * q : 32 * q + 4, :].bitcast(I32), tab_scales[0, 4 * q : 4 * q + 4, :].bitcast(I32))
        nc.sync.dma_start(called_list[:], offs2)
        load_rows(wb_raw[0], wb, 0)
        load_rows(wa_raw[0], wa, 0)
        load_rows(wb_raw[1], wb, K_PASS)
        nc.sync.dma_start(bh_sb[:], bh.rearrange("(b p t) -> p b t", p=P, t=PACK))
        load_rows(wa_raw[1], wa, K_PASS)
        load_rows(wd_raw[0], wd, 0)
        nc.sync.dma_start(we_w[:].bitcast(I32), we_words[0].rearrange("p n i -> p (n i)").bitcast(I32))
        for q in range(4):
            nc.sync.dma_start(we_s[32 * q : 32 * q + 4, :].bitcast(I32), we_scales[0, 4 * q : 4 * q + 4, :].bitcast(I32))
        with nc.allow_non_contiguous_dma(reason="one bias value for each partition and row tile"):
            nc.sync.dma_start(be_sb[:], be.rearrange("(m p) -> p m", p=P))
        nc.sync.dma_start(wc_w[:].bitcast(I32), wc_words.rearrange("a p n -> p a n").bitcast(I32))
        for q in range(4):
            nc.sync.dma_start(
                wc_s[32 * q : 32 * q + 4, :, :].bitcast(I32),
                wc_scales[:, 4 * q : 4 * q + 4, :].rearrange("a r n -> r a n").bitcast(I32),
            )
        nc.sync.dma_start(case_list[:], offs3)
        nc.sync.dma_start(wgo_sb[:], wgo)
        load_rows(wd_raw[1], wd, WD_EARLY)

        def gather(dst, window, lst, half):
            cols = BANK // 16
            nc.vector.tensor_copy(dst[:], window[:].indirect(lst[:, half * cols : (half + 1) * cols]))

        def reused(shape, dtype, name, slot):
            return shared.tile(shape, dtype, name=name, align_bytes=64, offset=slot * SLOT_BYTES)

        caller_w = [held([P, BANK], U32, f"caller_w{i}") for i in range(HALVES)]
        called_w = [held([P, BANK], U32, "called_w0")]
        caller_s = [held([P, BANK], U8, "caller_s0")]
        called_s = [held([P, BANK], U8, "called_s0")]
        gather(caller_w[0], tab_w, caller_list, 0)
        gather(called_w[0], tab_w, called_list, 0)
        gather(caller_s[0], tab_s, caller_list, 0)
        gather(called_s[0], tab_s, called_list, 0)
        gather(caller_w[1], tab_w, caller_list, 1)

        def gather_late(tiles, dtype, name, slot, window, lst):
            tiles.append(reused([P, BANK], dtype, name, slot))
            gather(tiles[1], window, lst, 1)

        def quantise(rounded, name):
            words = rounded.shape[1] // PACK
            codes = held([P, words], U32, name + "_w")
            scales = held([P, words], U8, name + "_s")
            nc.vector.quantize_mx(out=codes[:].bitcast(FP8X4), scales=scales[:], in_=rounded[:])
            return codes, scales

        def dealt_views(raw, rounded):
            return (
                rounded[:].rearrange("p (t m j) -> p m j t", t=PACK, j=PACK),
                raw[:].rearrange("p j (m t) -> p m j t", t=PACK),
            )

        wa_q, wb_q = [], []
        for b in range(H_PASSES):
            rounded = held([P, PACK * K_PASS], BF16, f"wb_bf{b}")
            nc.scalar.activation(*dealt_views(wb_raw[b], rounded), ACT.Copy, scale=-1.0)
            wb_q.append(quantise(rounded, f"wb_q{b}"))
            if b == 0:
                rounded = reused([P, PACK * K_PASS], BF16, "wa_bf0", 0)
                nc.scalar.copy(*dealt_views(wa_raw[b], rounded))
            else:
                rounded = held([P, PACK * K_PASS], BF16, "wa_bf1")
                nc.vector.tensor_copy(*dealt_views(wa_raw[b], rounded))
            wa_q.append(quantise(rounded, f"wa_q{b}"))
            if b == 0:
                gather_late(called_w, U32, "called_w1", 0, tab_w, called_list)

        def round_wd(i, rounded):
            nc.scalar.copy(
                rounded[:].rearrange("p (c i j) -> p c j i", i=4, j=PACK),
                wd_raw[i][:].rearrange("p j (c i) -> p c j i", i=4),
            )
            return quantise(rounded, f"wd_q{i}")

        h_w = [held([P, S], U32, f"h_w{b}") for b in range(H_PASSES)]
        h_s = [held([P, S], U8, f"h_s{b}") for b in range(H_PASSES)]
        h_woven = [
            [reused([P, PACK * BANK], BF16, f"h_woven{half}{b}", 1 + H_PASSES * half + b) for b in range(H_PASSES)]
            for half in range(HALVES)
        ]
        h_flat = [held([P, PACK, BANK], BF16, f"h_flat{b}") for b in range(H_PASSES)]

        def weave(copy, woven, flat):
            copy(
                woven[:].rearrange("p (c i t) -> p c t i", i=4, t=PACK),
                flat[:].rearrange("p t (c i) -> p c t i", i=4),
            )

        def make_h(half):
            cols = slice(half * BANK, (half + 1) * BANK)
            for b in range(H_PASSES):
                for t in range(PACK):
                    d = psum.tile([P, BANK], F32, name="d", bufs=4)
                    m_cols = slice(t * P, (t + 1) * P)
                    for (w, s), gw, gs, first in ((wa_q[b], caller_w, caller_s, True), (wb_q[b], called_w, called_s, False)):
                        nc.tensor.matmul_mx(
                            out=d[:],
                            lhsT=w[:, m_cols].bitcast(FP8X4),
                            lhsT_scale=s[:, m_cols],
                            rhs=gw[half][:].bitcast(FP8X4),
                            rhs_scale=gs[half][:],
                            start=first,
                            stop=not first,
                        )
                    nc.scalar.activation(h_flat[b][:, t, :], d[:], ACT.Abs, bias=bh_sb[:, b, t : t + 1])
                woven = h_woven[half][b]
                weave(nc.vector.tensor_copy if half == 0 else nc.scalar.copy, woven, h_flat[b])
                nc.vector.quantize_mx(out=h_w[b][:, cols].bitcast(FP8X4), scales=h_s[b][:, cols], in_=woven[:])

        ceilings = {}

        def make_ceiling(m, half):
            n_cols = slice(m * P, (m + 1) * P)
            top = psum.tile([P, BANK], F32, name="top", bufs=1)
            nc.tensor.matmul_mx(
                out=top[:],
                lhsT=we_w[:, n_cols].bitcast(FP8X4),
                lhsT_scale=we_s[:, n_cols],
                rhs=called_w[half][:].bitcast(FP8X4),
                rhs_scale=called_s[half][:],
                start=True,
                stop=True,
            )
            ceiling = held([P, BANK], F32, f"ceiling{m}{half}")
            nc.scalar.activation(ceiling[:], top[:], ACT.Identity, bias=be_sb[:, m : m + 1])
            ceilings[m, half] = ceiling

        def scores(m, half, y, order):
            cols = slice(half * BANK, (half + 1) * BANK)
            n_cols = slice(m * P, (m + 1) * P)
            if (m, half) not in ceilings:
                make_ceiling(m, half)
            e = psum.tile([P, BANK], F32, name="e", bufs=3)
            wd_w, wd_s = wd_q[m * P // WD_EARLY]
            wd_cols = slice(m * P % WD_EARLY, m * P % WD_EARLY + P)
            passes = [
                (
                    wc_w[:, b, 2 * m * P : 2 * (m + 1) * P].bitcast(FP4X4),
                    wc_s[:, b, n_cols],
                    h_w[b][:, cols].bitcast(FP8X4),
                    h_s[b][:, cols],
                )
                for b in range(H_PASSES)
            ]
            wd_pass = (
                wd_w[:, wd_cols].bitcast(FP8X4),
                wd_s[:, wd_cols],
                caller_w[half][:].bitcast(FP8X4),
                caller_s[half][:],
            )
            passes.append(wd_pass)
            for i, (lhsT, lhsT_scale, rhs, rhs_scale) in enumerate([passes[k] for k in order]):
                nc.tensor.matmul_mx(
                    out=e[:],
                    lhsT=lhsT,
                    lhsT_scale=lhsT_scale,
                    rhs=rhs,
                    rhs_scale=rhs_scale,
                    start=i == 0,
                    stop=i == len(passes) - 1,
                )
            nc.vector.tensor_tensor(y, e[:], ceilings[m, half][:], ALU.min)

        def place(m, cols, y):
            nc.vector.tensor_tensor(
                pages[m % PAGES][:].indirect(case_list[:, cols.start // 16 : cols.stop // 16]), y, wgo_sb[:, cols], ALU.mult
            )

        def store(m):
            nc.sync.dma_start(out[m * P : (m + 1) * P, :], pages[m % PAGES][:])

        make_h(0)
        wd_q = [round_wd(0, held([P, PACK * WD_EARLY], BF16, "wd_bf0"))]
        gather_late(caller_s, U8, "caller_s1", 1, tab_s, caller_list)
        gather_late(called_s, U8, "called_s1", 2, tab_s, called_list)

        def page_round(half):
            cols = slice(half * BANK, (half + 1) * BANK)
            ys = []
            for m in range(PAGES + 1):
                if m < PAGES:
                    ys.append(work.tile([P, BANK], F32, name="y_half", bufs=3))
                    scores(m, half, ys[m][:], (0, 2, 1) if half == 0 else (2, 1, 0) if m == 0 else (1, 0, 2))
                if m > 0:
                    place(m - 1, cols, ys[m - 1][:])
                    if half == HALVES - 1:
                        store(m - 1)

        page_round(0)
        make_h(1)
        y_rows = {PAGES: h_woven[1][1][:].bitcast(F32)}
        scores(PAGES, 0, y_rows[PAGES][:, 0:BANK], (2, 0, 1))
        page_round(1)
        wd_q.append(round_wd(1, h_flat[1][:].rearrange("p t n -> p (t n)")[:, 0 : PACK * (N - WD_EARLY)]))
        scores(PAGES, 1, y_rows[PAGES][:, BANK:S], (1, 0, 2))
        for m in range(PAGES, ROW_TILES):
            if m + 1 < ROW_TILES:
                y_rows[m + 1] = held([P, S], F32, f"y_row{m + 1}")[:]
                for half in range(HALVES):
                    scores(m + 1, half, y_rows[m + 1][:, half * BANK : (half + 1) * BANK], (2, 0, 1))
            place(m, slice(0, S), y_rows[m])
            store(m)
